import numpy as np
import ml_dtypes


def mxq(x, axis, fmt="e4m3"):
    dtype, down = {"e4m3": (ml_dtypes.float8_e4m3fn, 7), "e5m2": (ml_dtypes.float8_e5m2, 14)}[fmt]
    v = np.moveaxis(np.asarray(x, np.float32).astype(ml_dtypes.bfloat16).astype(np.float64), axis, -1)
    blocks = v.reshape(v.shape[:-1] + (-1, 32))
    amax = np.abs(blocks).max(-1, keepdims=True)
    byte = np.maximum(np.where(amax > 0, np.frexp(amax)[1] - 1 + 127, 0) - down, 1)
    scale = np.exp2(byte - 127.0)
    codes = (blocks / scale).astype(np.float32).astype(dtype).astype(np.float64)
    return np.moveaxis((codes * scale).reshape(v.shape), -1, axis)


WIDE = False


def mx_kscale(k):
    if not WIDE:
        return np.ones(k)
    levels = np.array([10, -10, 5, -5, 0])
    if k % 512:
        return np.exp2(np.random.permutation(np.resize(levels, k // 32))).repeat(32)
    a = np.empty((k // 512, 16))
    for p in range(k // 512):
        a[p, :8] = np.random.permutation(np.resize(levels, 8))
        for g in range(8):
            far = levels[np.abs(levels - a[p, g]) >= 10]
            a[p, g + 8] = far[np.random.randint(len(far))]
    return np.exp2(a.ravel()).repeat(32)


def f64(x):
    return np.asarray(x).astype(np.float64)


def striped8(idx):
    return np.asarray(idx).reshape(8, -1, 16).transpose(0, 2, 1).reshape(128, -1).astype(np.uint16)


def unstriped8(offs):
    return offs.reshape(8, 16, -1).transpose(0, 2, 1).reshape(8, -1).astype(np.int64)


def pick8(x, idx, run):
    r = np.arange(len(x))
    return x[r[:, None], idx[r % (8 * run) // run]]


E2M1 = np.array([0.0, 0.5, 1.0, 1.5, 2.0, 3.0, 4.0, 6.0, -0.0, -0.5, -1.0, -1.5, -2.0, -3.0, -4.0, -6.0])


def pack_weight(w, fmt):
    k, n = w.shape
    w = f64(np.asarray(w, np.float32).astype(ml_dtypes.bfloat16)).reshape(k // 32, 32, n)
    amax = np.abs(w).max(1)
    if fmt == "e4m3":
        byte = np.frexp(amax)[1] - 1 + 127 - 7
    else:
        mant, ex = np.frexp(amax / 6.0)
        byte = np.where(mant > 0.5, ex, ex - 1) + 127
    byte = np.clip(np.where(amax > 0, byte, 1), 1, 254)
    scaled = (w * np.exp2(127.0 - byte)[:, None, :]).reshape(k, n).astype(np.float32)
    by_word = np.ascontiguousarray(scaled.reshape(k // 512, 128, 4, n).transpose(0, 1, 3, 2))
    if fmt == "e4m3":
        words = by_word.astype(ml_dtypes.float8_e4m3fn).view(np.uint8)
    else:
        c = by_word.astype(ml_dtypes.float4_e2m1fn).view(np.uint8) & 0xF
        words = (c[..., 0::2] | (c[..., 1::2] << 4)).reshape(k // 512, 128, 2 * n)
    return np.ascontiguousarray(words), np.ascontiguousarray(byte.astype(np.uint8).reshape(k // 512, 16, n))


def unpack_weight(words, scales, fmt):
    g, _, n = scales.shape
    words = np.ascontiguousarray(words).reshape(g, 128, n, -1)
    if fmt == "e4m3":
        vals = words.view(ml_dtypes.float8_e4m3fn).astype(np.float64)
    else:
        nib = np.empty((g, 128, n, 4), np.uint8)
        nib[..., 0::2] = words & 0xF
        nib[..., 1::2] = words >> 4
        vals = E2M1[nib]
    vals = vals * np.repeat(np.exp2(scales.astype(np.float64) - 127.0), 8, axis=1)[..., None]
    return vals.transpose(0, 1, 3, 2).reshape(g * 512, n)


def bf(x):
    return np.asarray(x, np.float32).astype(ml_dtypes.bfloat16)


def planes(Y):
    r, m = Y.shape
    b = f64(bf(Y)).reshape(r // 32, 32, m)
    amax = np.abs(b).max(1)
    byte = np.clip(np.where(amax > 0, np.frexp(amax)[1] - 1 + 127 - 7, 1), 1, 254)
    codes = (b * np.exp2(127.0 - byte)[:, None, :]).reshape(r, m).astype(np.float32).astype(ml_dtypes.float8_e4m3fn).view(np.uint8)
    words = codes.reshape(r // 512, 128, 4, m).transpose(0, 1, 3, 2)
    return np.ascontiguousarray(words), np.ascontiguousarray(byte.astype(np.uint8).reshape(r // 512, 16, m))


K, T, J, N = 512, 1024, 512, 512


def setup_inputs():
    n = np.random.standard_normal
    idx = np.stack([np.random.permutation(T)[:J] for _ in range(8)])
    idx2 = np.stack([np.random.permutation(T)[:J] for _ in range(8)])
    fk = mx_kscale(K)
    wap = pack_weight(n((K, N)) * 1 / np.sqrt(K) * fk[:, None], "e2m1")
    wbp = pack_weight(n((K, N)) * 1 / np.sqrt(K) * fk[:, None], "e4m3")
    return {
        "xt": (n((K, T)) / fk[:, None]).astype(np.float32),
        "wa_words": wap[0],
        "wa_scales": wap[1],
        "wb_words": wbp[0],
        "wb_scales": wbp[1],
        "offs": striped8(idx),
        "offs2": striped8(idx2),
    }


def reference(xt, wa_words, wa_scales, wb_words, wb_scales, offs, offs2):
    idx = unstriped8(offs)
    idx2 = unstriped8(offs2)
    wau = unpack_weight(wa_words, wa_scales, "e2m1")
    wbu = unpack_weight(wb_words, wb_scales, "e4m3")
    xtidxq = mxq(pick8(f64(xt), idx, 64), 0, "e4m3")
    p = wau.T @ xtidxq
    xtidx2q = mxq(pick8(f64(xt), idx2, 64), 0, "e4m3")
    q = wbu.T @ xtidx2q
    y = np.maximum(p, q) - 0.3 * np.minimum(p, q)
    words, scales = planes(y)
    return y, words, scales

@@ -1,0 +1,215 @@
+from contextlib import ExitStack
+
+import concourse.mybir as mybir
+from concourse.masks import make_identity
+
+K, T, J, N = 512, 1024, 512, 512
+FLOPS = 2 * 2 * K * N * J
+
+F32 = mybir.dt.float32
+BF16 = mybir.dt.bfloat16
+I32 = mybir.dt.int32
+U32 = mybir.dt.uint32
+U16 = mybir.dt.uint16
+U8 = mybir.dt.uint8
+FP8X4 = mybir.dt.float8_e4m3fn_x4
+FP4X4 = mybir.dt.float4_e2m1fn_x4
+COPY = mybir.ActivationFunctionType.Copy
+MULT = mybir.AluOpType.mult
+ADD = mybir.AluOpType.add
+MAX = mybir.AluOpType.max
+
+P = 128
+SLOTS = 128
+TILES = J // SLOTS
+SMALL = -0.3
+
+LOW_CUTS = (0, 512, 1024)
+HIGH_CUTS = (0, 256, 640, 1024)
+
+
+def tile_moe_expert_heads_twice_pl_kernel(tc, xt, wa_words, wa_scales, wb_words, wb_scales, offs, offs2, out_0, out_1, out_2):
+    nc = tc.nc
+    with ExitStack() as ctx:
+        sb = ctx.enter_context(tc.tile_pool(name="sb", bufs=1))
+        ps = ctx.enter_context(tc.psum_pool(name="ps", bufs=1))
+
+        lists = [sb.tile([P, J // 16], U16, name="list%d" % e) for e in range(2)]
+        cuts = (LOW_CUTS, HIGH_CUTS)
+        raw = [[sb.tile([P, 2, cuts[h][i + 1] - cuts[h][i]], F32, name="raw%d%d" % (h, i)) for i in range(len(cuts[h]) - 1)] for h in range(2)]
+        pairs = [sb.tile([P, T], U32, name="pairs%d" % h) for h in range(2)]
+        wa = sb.tile([P, 2 * N], U8, name="wa", align_bytes=64)
+        wb = sb.tile([P, 4 * N], U8, name="wb", align_bytes=64)
+        wa_plane = sb.tile([P, N], U8, name="wa_plane", align_bytes=64)
+        wb_plane = sb.tile([P, N], U8, name="wb_plane", align_bytes=64)
+        ident = sb.tile([P, P], F32, name="ident")
+        y_words = sb.tile([P, J], U32, name="y_words", align_bytes=64)
+        y_plane = sb.tile([P, J], U8, name="y_plane", align_bytes=64)
+
+        x_rows = xt.rearrange("(p t) c -> p t c", t=4)
+
+        def load_x(h, i):
+            nc.sync.dma_start(out=raw[h][i][:], in_=x_rows[:, 2 * h : 2 * h + 2, cuts[h][i] : cuts[h][i + 1]])
+
+        def load_scales(queue, plane, scales, q):
+            queue.dma_start(out=plane[32 * q : 32 * q + 4, :].bitcast(I32), in_=scales[0, 4 * q : 4 * q + 4, :].bitcast(I32))
+
+        nc.vector.memset(wa_plane[:].bitcast(I32), 0)
+        nc.vector.memset(wb_plane[:].bitcast(I32), 0)
+        load_x(0, 0)
+        nc.sync.dma_start(lists[0][:], offs)
+        nc.sync.dma_start(lists[1][:], offs2)
+        load_x(0, 1)
+        for i in range(len(HIGH_CUTS) - 1):
+            load_x(1, i)
+        nc.sync.dma_start(out=wb[:].bitcast(I32), in_=wb_words[0].rearrange("p n t -> p (n t)").bitcast(I32))
+        nc.sync.dma_start(out=wa[:].bitcast(I32), in_=wa_words[0].bitcast(I32))
+        for q in range(4):
+            load_scales(nc.sync, wb_plane, wb_scales, q)
+        for q in range(4):
+            load_scales(nc.sync if q < 2 else nc.gpsimd, wa_plane, wa_scales, q)
+        make_identity(nc, ident[:])
+
+        def pair_up(engine, h, i, lo, hi):
+            dst = pairs[h][:].bitcast(BF16).rearrange("p (c e) -> p c e", e=2)[:, lo:hi, :]
+            src = raw[h][i][:, :, lo - cuts[h][i] : hi - cuts[h][i]].rearrange("p e c -> p c e")
+            if engine == "vector":
+                nc.vector.tensor_copy(out=dst, in_=src)
+            else:
+                nc.scalar.activation(out=dst, in_=src, func=COPY)
+
+        pair_up("vector", 0, 0, 0, 512)
+        pair_up("scalar", 0, 1, 512, 672)
+        pair_up("vector", 0, 1, 672, 1024)
+        for i in range(len(HIGH_CUTS) - 1):
+            pair_up("scalar", 1, i, HIGH_CUTS[i], HIGH_CUTS[i + 1])
+
+        W = 2 * SLOTS
+        shared = [sb.tile([P, 3 * W], U32, name="shared%d" % c, align_bytes=64) for c in range(2)]
+        picked = [sb.tile([P, 2 * W], U32, name="picked%d" % c)[:] for c in range(2)] + [shared[c][:, : 2 * W] for c in range(2)]
+        quads = [shared[c][:, W:] for c in range(2)] + [sb.tile([P, 2 * W], U32, name="quads%d" % c, align_bytes=64)[:] for c in range(2)]
+
+        def gather(h, c):
+            for e in range(2):
+                lo = h * W + e * SLOTS
+                nc.vector.tensor_copy(out=picked[c][:, lo : lo + SLOTS], in_=pairs[h][:].indirect(lists[e][:, c * 8 : (c + 1) * 8]))
+
+        for c in range(TILES):
+            gather(0, c)
+
+        x_words = [sb.tile([P, W], U32, name="x_words%d" % c, align_bytes=64) for c in range(TILES)]
+        x_plane = [sb.tile([P, W], U8, name="x_plane%d" % c, align_bytes=64) for c in range(TILES)]
+        y_rows = out_0.rearrange("(p t) j -> p t j", t=4)
+        p_banks, q_banks, q_small, p_small, y_banks, y_quads = {}, {}, {}, {}, {}, {}
+        ys = [sb.tile([P, 4, SLOTS], F32, name="y%d" % c) for c in range(TILES)]
+
+        def weave(c, engine):
+            src = picked[c].rearrange("p (h s) -> p s h", h=2)
+            dst = quads[c].rearrange("p (s h) -> p s h", h=2)
+            if engine == "vector":
+                nc.vector.tensor_copy(out=dst.bitcast(I32), in_=src.bitcast(I32))
+            else:
+                nc.scalar.copy(out=dst, in_=src)
+
+        def quantise_x(c):
+            nc.vector.quantize_mx(out=x_words[c][:].bitcast(FP8X4), scales=x_plane[c][:], in_=quads[c].bitcast(BF16))
+
+        def multiply(c):
+            p_banks[c] = ps.tile([P, N], F32, name="p_bank", tag="p", bufs=4)
+            q_banks[c] = ps.tile([P, N], F32, name="q_bank", tag="q", bufs=2)
+            nc.tensor.matmul_mx(out=q_banks[c][:], lhsT=x_words[c][:, SLOTS:].bitcast(FP8X4), lhsT_scale=x_plane[c][:, SLOTS:],
+                                rhs=wb[:].bitcast(FP8X4), rhs_scale=wb_plane[:], start=True, stop=True)
+            nc.tensor.matmul_mx(out=p_banks[c][:], lhsT=x_words[c][:, :SLOTS].bitcast(FP8X4), lhsT_scale=x_plane[c][:, :SLOTS],
+                                rhs=wa[:].bitcast(FP4X4), rhs_scale=wa_plane[:], start=True, stop=True)
+
+        def dealt(bank):
+            return bank[:].rearrange("j (m t) -> j t m", t=4)
+
+        def scale_q(c):
+            q_small[c] = sb.tile([P, 4, P], F32, name="q_small%d" % c)
+            nc.scalar.activation(out=q_small[c][:], in_=dealt(q_banks[c]), func=COPY, scale=SMALL)
+
+        def turn(c, ts, tag, terms):
+            count = ts.stop - ts.start
+            y_bank = ps.tile([P, count, SLOTS], F32, name="y_bank", tag=tag, bufs=2)
+            for i, term in enumerate(terms):
+                for t in range(count):
+                    nc.tensor.matmul(out=y_bank[:, t, :], lhsT=term[:, t, :], rhs=ident[:], is_transpose=True,
+                                     start=(i == 0 and t == 0), stop=(i == len(terms) - 1 and t == count - 1))
+            y_banks[c, ts.start] = y_bank
+
+        def combine(c, ts, tag):
+            count = ts.stop - ts.start
+            lesser = sb.tile([P, count, P], F32, name="lesser%d%d" % (c, ts.start))
+            greater = sb.tile([P, count, P], F32, name="greater%d%d" % (c, ts.start))
+            p_dealt = dealt(p_banks[c])[:, ts, :]
+            nc.vector.scalar_tensor_tensor(out=lesser[:], in0=p_dealt, scalar=SMALL, in1=q_small[c][:, ts, :], op0=MULT, op1=MAX)
+            nc.vector.scalar_tensor_tensor(out=greater[:], in0=q_small[c][:, ts, :], scalar=1.0 / SMALL, in1=p_dealt, op0=MULT, op1=MAX)
+            turn(c, ts, tag, (lesser, greater))
+
+        def copy_y(c, ts):
+            nc.scalar.copy(out=ys[c][:, ts, :], in_=y_banks[c, ts.start][:])
+            nc.sync.dma_start(out=y_rows[:, ts, c * SLOTS : (c + 1) * SLOTS], in_=ys[c][:, ts, :])
+
+        def round_y(c, engine):
+            y_quads[c] = sb.tile([P, SLOTS, 4], BF16, name="y_quads%d" % c, align_bytes=64)
+            src = ys[c][:].rearrange("p t j -> p j t")
+            if engine == "vector":
+                nc.vector.tensor_copy(out=y_quads[c][:], in_=src)
+            elif engine == "gpsimd":
+                nc.gpsimd.tensor_scalar(out=y_quads[c][:], in0=src, scalar1=1.0, scalar2=0.0, op0=MULT, op1=ADD)
+            else:
+                nc.scalar.copy(out=y_quads[c][:], in_=src)
+
+        def quantise_y(c):
+            cols = slice(c * SLOTS, (c + 1) * SLOTS)
+            nc.vector.quantize_mx(out=y_words[:, cols].bitcast(FP8X4), scales=y_plane[:, cols],
+                                  in_=y_quads[c][:].rearrange("p j t -> p (j t)"))
+
+        def store_words(c0, c1):
+            cols = slice(c0 * SLOTS, c1 * SLOTS)
+            nc.sync.dma_start(out=out_1[0].rearrange("p j t -> p (j t)").bitcast(I32)[:, cols], in_=y_words[:, cols].bitcast(I32))
+
+        whole, low, high = slice(0, 4), slice(0, 2), slice(2, 4)
+
+        gather(1, 0)
+        weave(0, "scalar")
+        gather(1, 1)
+        weave(1, "scalar")
+        quantise_x(0)
+        multiply(0)
+        gather(1, 2)
+        weave(2, "scalar")
+        quantise_x(1)
+        multiply(1)
+        scale_q(0)
+        gather(1, 3)
+        weave(3, "scalar")
+        quantise_x(2)
+        multiply(2)
+        scale_q(1)
+        combine(0, whole, "y")
+        quantise_x(3)
+        multiply(3)
+        scale_q(2)
+        combine(1, whole, "y")
+        copy_y(0, whole)
+        scale_q(3)
+        round_y(0, "scalar")
+        combine(2, whole, "y")
+        copy_y(1, whole)
+        quantise_y(0)
+        round_y(1, "scalar")
+        combine(3, whole, "y")
+        copy_y(2, whole)
+        quantise_y(1)
+        round_y(2, "vector")
+        quantise_y(2)
+        store_words(0, 3)
+        copy_y(3, whole)
+        round_y(3, "vector")
+        quantise_y(3)
+        store_words(3, 4)
+        for q in range(4):
+            queue = nc.sync if q % 2 == 0 else nc.scalar
+            queue.dma_start(out=out_2[0, 4 * q : 4 * q + 4, :].bitcast(I32), in_=y_plane[32 * q : 32 * q + 4, :].bitcast(I32))

@@ -123,43 +123,41 @@ def tile_moe_expert_heads_twice_pl_kernel(tc, xt, wa_words, wa_scales, wb_words,
                                 rhs=wa[:].bitcast(FP4X4), rhs_scale=wa_plane[:], start=True, stop=True)
 
         def dealt(bank):
-            return bank[:].rearrange("j (m t) -> j t m", t=4)
+            return bank[:].rearrange("j (m u e) -> j u m e", u=2, e=2)
 
         def scale_q(c):
-            q_small[c] = sb.tile([P, 4, P], F32, name="q_small%d" % c)
+            q_small[c] = sb.tile([P, 2, P, 2], F32, name="q_small%d" % c)
             nc.scalar.activation(out=q_small[c][:], in_=dealt(q_banks[c]), func=COPY, scale=SMALL)
 
-        def turn(c, ts, tag, terms):
-            count = ts.stop - ts.start
-            y_bank = ps.tile([P, count, SLOTS], F32, name="y_bank", tag=tag, bufs=2)
-            for i, term in enumerate(terms):
-                for t in range(count):
-                    nc.tensor.matmul(out=y_bank[:, t, :], lhsT=term[:, t, :], rhs=ident[:], is_transpose=True,
-                                     start=(i == 0 and t == 0), stop=(i == len(terms) - 1 and t == count - 1))
-            y_banks[c, ts.start] = y_bank
+        def combine(c, us, tag):
+            y_bank = ps.tile([P, 2 * len(us), SLOTS], F32, name="y_bank", tag=tag, bufs=2)
+            for u in us:
+                lesser = sb.tile([P, P, 2], F32, name="lesser%d%d" % (c, u))
+                greater = sb.tile([P, P, 2], F32, name="greater%d%d" % (c, u))
+                p_dealt = dealt(p_banks[c])[:, u]
+                nc.vector.scalar_tensor_tensor(out=lesser[:], in0=p_dealt, scalar=SMALL, in1=q_small[c][:, u], op0=MULT, op1=MAX)
+                nc.vector.scalar_tensor_tensor(out=greater[:], in0=q_small[c][:, u], scalar=1.0 / SMALL, in1=p_dealt, op0=MULT, op1=MAX)
+                for i, term in enumerate((lesser, greater)):
+                    for e in range(2):
+                        nc.tensor.matmul(out=y_bank[:, 2 * (u - us[0]) + e, :], lhsT=term[:, :, e], rhs=ident[:], is_transpose=True,
+                                         start=(u == us[0] and i == 0 and e == 0), stop=(u == us[-1] and i == 1 and e == 1))
+            y_banks[c, us[0]] = y_bank
 
-        def combine(c, ts, tag):
-            count = ts.stop - ts.start
-            lesser = sb.tile([P, count, P], F32, name="lesser%d%d" % (c, ts.start))
-            greater = sb.tile([P, count, P], F32, name="greater%d%d" % (c, ts.start))
-            p_dealt = dealt(p_banks[c])[:, ts, :]
-            nc.vector.scalar_tensor_tensor(out=lesser[:], in0=p_dealt, scalar=SMALL, in1=q_small[c][:, ts, :], op0=MULT, op1=MAX)
-            nc.vector.scalar_tensor_tensor(out=greater[:], in0=q_small[c][:, ts, :], scalar=1.0 / SMALL, in1=p_dealt, op0=MULT, op1=MAX)
-            turn(c, ts, tag, (lesser, greater))
-
-        def copy_y(c, ts):
-            nc.scalar.copy(out=ys[c][:, ts, :], in_=y_banks[c, ts.start][:])
+        def copy_y(c, us):
+            ts = slice(2 * us[0], 2 * us[-1] + 2)
+            nc.scalar.copy(out=ys[c][:, ts, :], in_=y_banks[c, us[0]][:])
             nc.sync.dma_start(out=y_rows[:, ts, c * SLOTS : (c + 1) * SLOTS], in_=ys[c][:, ts, :])
 
         def round_y(c, engine):
             y_quads[c] = sb.tile([P, SLOTS, 4], BF16, name="y_quads%d" % c, align_bytes=64)
-            src = ys[c][:].rearrange("p t j -> p j t")
+            src = ys[c][:].rearrange("p t (b i) -> p b t i", i=4)
+            dst = y_quads[c][:].rearrange("p (b i) t -> p b t i", i=4)
             if engine == "vector":
-                nc.vector.tensor_copy(out=y_quads[c][:], in_=src)
+                nc.vector.tensor_copy(out=dst, in_=src)
             elif engine == "gpsimd":
-                nc.gpsimd.tensor_scalar(out=y_quads[c][:], in0=src, scalar1=1.0, scalar2=0.0, op0=MULT, op1=ADD)
+                nc.gpsimd.tensor_scalar(out=dst, in0=src, scalar1=1.0, scalar2=0.0, op0=MULT, op1=ADD)
             else:
-                nc.scalar.copy(out=y_quads[c][:], in_=src)
+                nc.scalar.copy(out=dst, in_=src)
 
         def quantise_y(c):
             cols = slice(c * SLOTS, (c + 1) * SLOTS)
@@ -170,7 +168,7 @@ def tile_moe_expert_heads_twice_pl_kernel(tc, xt, wa_words, wa_scales, wb_words,
             cols = slice(c0 * SLOTS, c1 * SLOTS)
             nc.sync.dma_start(out=out_1[0].rearrange("p j t -> p (j t)").bitcast(I32)[:, cols], in_=y_words[:, cols].bitcast(I32))
 
-        whole, low, high = slice(0, 4), slice(0, 2), slice(2, 4)
+        whole, low, high = (0, 1), (0,), (1,)
 
         gather(1, 0)
         weave(0, "scalar")
@@ -198,18 +196,20 @@ def tile_moe_expert_heads_twice_pl_kernel(tc, xt, wa_words, wa_scales, wb_words,
         round_y(0, "scalar")
         combine(2, whole, "y")
         copy_y(1, whole)
-        quantise_y(0)
         round_y(1, "scalar")
-        combine(3, whole, "y")
+        combine(3, low, "q")
+        combine(3, high, "q")
         copy_y(2, whole)
+        quantise_y(0)
         quantise_y(1)
+        store_words(0, 2)
+        copy_y(3, low)
         round_y(2, "vector")
+        copy_y(3, high)
         quantise_y(2)
-        store_words(0, 3)
-        copy_y(3, whole)
         round_y(3, "vector")
         quantise_y(3)
-        store_words(3, 4)
+        store_words(2, 4)
         for q in range(4):
             queue = nc.sync if q % 2 == 0 else nc.scalar
             queue.dma_start(out=out_2[0, 4 * q : 4 * q + 4, :].bitcast(I32), in_=y_plane[32 * q : 32 * q + 4, :].bitcast(I32))

@@ -23,9 +23,11 @@ P = 128
 SLOTS = 128
 TILES = J // SLOTS
 SMALL = -0.3
+GAIN = 1.0 - SMALL
+THREE = (2,)
 
 LOW_CUTS = (0, 512, 1024)
-HIGH_CUTS = (0, 256, 640, 1024)
+HIGH_CUTS = (0, 384, 768, 1024)
 
 
 def tile_moe_expert_heads_twice_pl_kernel(tc, xt, wa_words, wa_scales, wb_words, wb_scales, offs, offs2, out_0, out_1, out_2):
@@ -43,7 +45,6 @@ def tile_moe_expert_heads_twice_pl_kernel(tc, xt, wa_words, wa_scales, wb_words,
         wa_plane = sb.tile([P, N], U8, name="wa_plane", align_bytes=64)
         wb_plane = sb.tile([P, N], U8, name="wb_plane", align_bytes=64)
         ident = sb.tile([P, P], F32, name="ident")
-        y_words = sb.tile([P, J], U32, name="y_words", align_bytes=64)
         y_plane = sb.tile([P, J], U8, name="y_plane", align_bytes=64)
 
         x_rows = xt.rearrange("(p t) c -> p t c", t=4)
@@ -54,20 +55,20 @@ def tile_moe_expert_heads_twice_pl_kernel(tc, xt, wa_words, wa_scales, wb_words,
         def load_scales(queue, plane, scales, q):
             queue.dma_start(out=plane[32 * q : 32 * q + 4, :].bitcast(I32), in_=scales[0, 4 * q : 4 * q + 4, :].bitcast(I32))
 
-        nc.vector.memset(wa_plane[:].bitcast(I32), 0)
-        nc.vector.memset(wb_plane[:].bitcast(I32), 0)
-        load_x(0, 0)
+        nc.gpsimd.memset(wb_plane[:].bitcast(I32), 0)
+        nc.gpsimd.memset(wa_plane[:].bitcast(I32), 0)
         nc.sync.dma_start(lists[0][:], offs)
+        load_x(0, 0)
         nc.sync.dma_start(lists[1][:], offs2)
+        for q in range(4):
+            load_scales(nc.sync, wb_plane, wb_scales, q)
         load_x(0, 1)
         for i in range(len(HIGH_CUTS) - 1):
             load_x(1, i)
         nc.sync.dma_start(out=wb[:].bitcast(I32), in_=wb_words[0].rearrange("p n t -> p (n t)").bitcast(I32))
         nc.sync.dma_start(out=wa[:].bitcast(I32), in_=wa_words[0].bitcast(I32))
         for q in range(4):
-            load_scales(nc.sync, wb_plane, wb_scales, q)
-        for q in range(4):
-            load_scales(nc.sync if q < 2 else nc.gpsimd, wa_plane, wa_scales, q)
+            load_scales(nc.sync, wa_plane, wa_scales, q)
         make_identity(nc, ident[:])
 
         def pair_up(engine, h, i, lo, hi):
@@ -85,27 +86,30 @@ def tile_moe_expert_heads_twice_pl_kernel(tc, xt, wa_words, wa_scales, wb_words,
             pair_up("scalar", 1, i, HIGH_CUTS[i], HIGH_CUTS[i + 1])
 
         W = 2 * SLOTS
-        shared = [sb.tile([P, 3 * W], U32, name="shared%d" % c, align_bytes=64) for c in range(2)]
-        picked = [sb.tile([P, 2 * W], U32, name="picked%d" % c)[:] for c in range(2)] + [shared[c][:, : 2 * W] for c in range(2)]
-        quads = [shared[c][:, W:] for c in range(2)] + [sb.tile([P, 2 * W], U32, name="quads%d" % c, align_bytes=64)[:] for c in range(2)]
+        picked = [sb.tile([P, 4 * W], U32, name="picked%d" % g, align_bytes=64) for g in range(2)]
+        quads = {0: picked[1][:, 2 * W :]}
 
-        def gather(h, c):
+        def gather(h, c, count=1):
             for e in range(2):
-                lo = h * W + e * SLOTS
-                nc.vector.tensor_copy(out=picked[c][:, lo : lo + SLOTS], in_=pairs[h][:].indirect(lists[e][:, c * 8 : (c + 1) * 8]))
+                lo = h * 2 * W + e * W + c % 2 * SLOTS
+                nc.vector.tensor_copy(out=picked[c // 2][:, lo : lo + count * SLOTS],
+                                      in_=pairs[h][:].indirect(lists[e][:, c * 8 : (c + count) * 8]))
 
-        for c in range(TILES):
-            gather(0, c)
+        gather(0, 0, 2)
+        gather(0, 2, 2)
 
-        x_words = [sb.tile([P, W], U32, name="x_words%d" % c, align_bytes=64) for c in range(TILES)]
+        x_words = [sb.tile([P, W], U32, name="x_words%d" % c, tag="words%d" % c, align_bytes=64) for c in range(TILES)]
         x_plane = [sb.tile([P, W], U8, name="x_plane%d" % c, align_bytes=64) for c in range(TILES)]
         y_rows = out_0.rearrange("(p t) j -> p t j", t=4)
-        p_banks, q_banks, q_small, p_small, y_banks, y_quads = {}, {}, {}, {}, {}, {}
+        p_banks, q_banks, q_small, y_banks = {}, {}, {}, {}
+        y_quads = [sb.tile([P, W, 4], BF16, name="y_quads%d" % g, align_bytes=64) for g in range(2)]
         ys = [sb.tile([P, 4, SLOTS], F32, name="y%d" % c) for c in range(TILES)]
 
-        def weave(c, engine):
-            src = picked[c].rearrange("p (h s) -> p s h", h=2)
-            dst = quads[c].rearrange("p (s h) -> p s h", h=2)
+        def weave(c, engine, tag=None, es=slice(0, 2)):
+            if tag is not None:
+                quads[c] = sb.tile([P, 2 * W], U32, name="quads%d" % c, tag=tag, align_bytes=64)[:]
+            src = picked[c // 2][:].rearrange("p (h e j) -> p e j h", h=2, e=2)[:, es, c % 2 * SLOTS : (c % 2 + 1) * SLOTS, :]
+            dst = quads[c].rearrange("p (e j h) -> p e j h", h=2, e=2)[:, es]
             if engine == "vector":
                 nc.vector.tensor_copy(out=dst.bitcast(I32), in_=src.bitcast(I32))
             else:
@@ -115,43 +119,56 @@ def tile_moe_expert_heads_twice_pl_kernel(tc, xt, wa_words, wa_scales, wb_words,
             nc.vector.quantize_mx(out=x_words[c][:].bitcast(FP8X4), scales=x_plane[c][:], in_=quads[c].bitcast(BF16))
 
         def multiply(c):
-            p_banks[c] = ps.tile([P, N], F32, name="p_bank", tag="p", bufs=4)
-            q_banks[c] = ps.tile([P, N], F32, name="q_bank", tag="q", bufs=2)
+            p_banks[c] = ps.tile([P, N], F32, name="p_bank", tag="p%d" % c)
+            q_banks[c] = ps.tile([P, N], F32, name="q_bank", tag="q%d" % c)
             nc.tensor.matmul_mx(out=q_banks[c][:], lhsT=x_words[c][:, SLOTS:].bitcast(FP8X4), lhsT_scale=x_plane[c][:, SLOTS:],
                                 rhs=wb[:].bitcast(FP8X4), rhs_scale=wb_plane[:], start=True, stop=True)
             nc.tensor.matmul_mx(out=p_banks[c][:], lhsT=x_words[c][:, :SLOTS].bitcast(FP8X4), lhsT_scale=x_plane[c][:, :SLOTS],
                                 rhs=wa[:].bitcast(FP4X4), rhs_scale=wa_plane[:], start=True, stop=True)
 
         def dealt(bank):
-            return bank[:].rearrange("j (m u e) -> j u m e", u=2, e=2)
+            return bank[:].rearrange("j (m t) -> j t m", t=4)
 
         def scale_q(c):
-            q_small[c] = sb.tile([P, 2, P, 2], F32, name="q_small%d" % c)
-            nc.scalar.activation(out=q_small[c][:], in_=dealt(q_banks[c]), func=COPY, scale=SMALL)
+            q_small[c] = sb.tile([P, 4, P], F32, name="q_small%d" % c)
+            nc.scalar.activation(out=q_small[c][:], in_=dealt(q_banks[c]), func=COPY, scale=SMALL / GAIN if c in THREE else SMALL)
 
-        def combine(c, us, tag):
-            y_bank = ps.tile([P, 2 * len(us), SLOTS], F32, name="y_bank", tag=tag, bufs=2)
-            for u in us:
-                lesser = sb.tile([P, P, 2], F32, name="lesser%d%d" % (c, u))
-                greater = sb.tile([P, P, 2], F32, name="greater%d%d" % (c, u))
-                p_dealt = dealt(p_banks[c])[:, u]
-                nc.vector.scalar_tensor_tensor(out=lesser[:], in0=p_dealt, scalar=SMALL, in1=q_small[c][:, u], op0=MULT, op1=MAX)
-                nc.vector.scalar_tensor_tensor(out=greater[:], in0=q_small[c][:, u], scalar=1.0 / SMALL, in1=p_dealt, op0=MULT, op1=MAX)
-                for i, term in enumerate((lesser, greater)):
-                    for e in range(2):
-                        nc.tensor.matmul(out=y_bank[:, 2 * (u - us[0]) + e, :], lhsT=term[:, :, e], rhs=ident[:], is_transpose=True,
-                                         start=(u == us[0] and i == 0 and e == 0), stop=(u == us[-1] and i == 1 and e == 1))
-            y_banks[c, us[0]] = y_bank
+        def turn(c, ts, term, first, last):
+            count = ts.stop - ts.start
+            for t in range(count):
+                nc.tensor.matmul(out=y_banks[c, ts.start][:, t, :], lhsT=term[:, t, :], rhs=ident[:], is_transpose=True,
+                                 start=(first and t == 0), stop=(last and t == count - 1))
 
-        def copy_y(c, us):
-            ts = slice(2 * us[0], 2 * us[-1] + 2)
-            nc.scalar.copy(out=ys[c][:, ts, :], in_=y_banks[c, us[0]][:])
+        def lesser(c, ts, tag):
+            count = ts.stop - ts.start
+            term = sb.tile([P, count, P], F32, name="lesser%d%d" % (c, ts.start))
+            nc.vector.scalar_tensor_tensor(out=term[:], in0=dealt(p_banks[c])[:, ts, :], scalar=SMALL, in1=q_small[c][:, ts, :], op0=MULT, op1=MAX)
+            y_banks[c, ts.start] = ps.tile([P, count, SLOTS], F32, name="y_bank", tag=tag)
+            turn(c, ts, term, True, False)
+
+        def scale_p(c, tag):
+            term = sb.tile([P, 4, P], F32, name="p_small%d" % c)
+            nc.scalar.activation(out=term[:], in_=dealt(p_banks[c]), func=COPY, scale=SMALL / GAIN)
+            y_banks[c, 0] = ps.tile([P, 4, SLOTS], F32, name="y_bank", tag=tag)
+            turn(c, whole, q_small[c], True, False)
+            turn(c, whole, term, False, False)
+
+        def greater(c, ts):
+            count = ts.stop - ts.start
+            term = sb.tile([P, count, P], F32, name="greater", tag="greater%d%d" % (c, ts.start), align_bytes=64)
+            nc.vector.scalar_tensor_tensor(out=term[:], in0=q_small[c][:, ts, :], scalar=GAIN / SMALL if c in THREE else 1.0 / SMALL, in1=dealt(p_banks[c])[:, ts, :], op0=MULT, op1=MAX)
+            turn(c, ts, term, False, True)
+
+        def copy_y(c, ts):
+            if c in THREE:
+                nc.scalar.activation(out=ys[c][:, ts, :], in_=y_banks[c, ts.start][:], func=COPY, scale=GAIN)
+            else:
+                nc.scalar.copy(out=ys[c][:, ts, :], in_=y_banks[c, ts.start][:])
             nc.sync.dma_start(out=y_rows[:, ts, c * SLOTS : (c + 1) * SLOTS], in_=ys[c][:, ts, :])
 
         def round_y(c, engine):
-            y_quads[c] = sb.tile([P, SLOTS, 4], BF16, name="y_quads%d" % c, align_bytes=64)
             src = ys[c][:].rearrange("p t (b i) -> p b t i", i=4)
-            dst = y_quads[c][:].rearrange("p (b i) t -> p b t i", i=4)
+            dst = y_quads[c // 2][:, c % 2 * SLOTS : (c % 2 + 1) * SLOTS, :].rearrange("p (b i) t -> p b t i", i=4)
             if engine == "vector":
                 nc.vector.tensor_copy(out=dst, in_=src)
             elif engine == "gpsimd":
@@ -159,57 +176,62 @@ def tile_moe_expert_heads_twice_pl_kernel(tc, xt, wa_words, wa_scales, wb_words,
             else:
                 nc.scalar.copy(out=dst, in_=src)
 
-        def quantise_y(c):
-            cols = slice(c * SLOTS, (c + 1) * SLOTS)
-            nc.vector.quantize_mx(out=y_words[:, cols].bitcast(FP8X4), scales=y_plane[:, cols],
-                                  in_=y_quads[c][:].rearrange("p j t -> p (j t)"))
+        def round_half(c, ts, src):
+            dst = y_quads[c // 2][:, c % 2 * SLOTS : (c % 2 + 1) * SLOTS, ts]
+            nc.vector.tensor_copy(out=dst, in_=src.rearrange("p t j -> p j t"))
 
-        def store_words(c0, c1):
-            cols = slice(c0 * SLOTS, c1 * SLOTS)
+        def quantise_y(g):
+            cols = slice(g * W, (g + 1) * W)
+            nc.vector.quantize_mx(out=y_words[:, cols].bitcast(FP8X4), scales=y_plane[:, cols],
+                                  in_=y_quads[g][:].rearrange("p j t -> p (j t)"))
             nc.sync.dma_start(out=out_1[0].rearrange("p j t -> p (j t)").bitcast(I32)[:, cols], in_=y_words[:, cols].bitcast(I32))
 
-        whole, low, high = (0, 1), (0,), (1,)
+        whole, low, high = slice(0, 4), slice(0, 2), slice(2, 4)
 
         gather(1, 0)
-        weave(0, "scalar")
+        weave(0, "scalar", es=slice(0, 1))
+        weave(0, "scalar", es=slice(1, 2))
         gather(1, 1)
-        weave(1, "scalar")
+        weave(1, "scalar", "quads1")
         quantise_x(0)
         multiply(0)
         gather(1, 2)
-        weave(2, "scalar")
+        weave(2, "scalar", "quads2")
         quantise_x(1)
         multiply(1)
         scale_q(0)
         gather(1, 3)
-        weave(3, "scalar")
+        weave(3, "scalar", "quads3")
         quantise_x(2)
         multiply(2)
         scale_q(1)
-        combine(0, whole, "y")
+        lesser(0, whole, "q0")
         quantise_x(3)
         multiply(3)
+        greater(0, whole)
         scale_q(2)
-        combine(1, whole, "y")
+        scale_p(2, "q2")
+        lesser(1, whole, "q1")
+        greater(1, whole)
         copy_y(0, whole)
+        round_y(0, "gpsimd")
         scale_q(3)
-        round_y(0, "scalar")
-        combine(2, whole, "y")
+        greater(2, whole)
         copy_y(1, whole)
-        round_y(1, "scalar")
-        combine(3, low, "q")
-        combine(3, high, "q")
+        round_y(1, "gpsimd")
+        lesser(3, low, "q3")
+        greater(3, low)
+        lesser(3, high, "p0")
+        greater(3, high)
+        y_words = sb.tile([P, J], U32, name="y_words", tag="greater32", align_bytes=64)
         copy_y(2, whole)
+        round_y(2, "scalar")
+        round_half(3, low, y_banks[3, 0][:])
+        round_half(3, high, y_banks[3, 2][:])
+        copy_y(3, low)
+        copy_y(3, high)
         quantise_y(0)
         quantise_y(1)
-        store_words(0, 2)
-        copy_y(3, low)
-        round_y(2, "vector")
-        copy_y(3, high)
-        quantise_y(2)
-        round_y(3, "vector")
-        quantise_y(3)
-        store_words(2, 4)
         for q in range(4):
             queue = nc.sync if q % 2 == 0 else nc.scalar
             queue.dma_start(out=out_2[0, 4 * q : 4 * q + 4, :].bitcast(I32), in_=y_plane[32 * q : 32 * q + 4, :].bitcast(I32))

from contextlib import ExitStack

import concourse.mybir as mybir
from concourse.masks import make_identity

K, T, J, N = 512, 1024, 512, 512
FLOPS = 2 * 2 * K * N * J

F32 = mybir.dt.float32
BF16 = mybir.dt.bfloat16
I32 = mybir.dt.int32
U32 = mybir.dt.uint32
U16 = mybir.dt.uint16
U8 = mybir.dt.uint8
FP8X4 = mybir.dt.float8_e4m3fn_x4
FP4X4 = mybir.dt.float4_e2m1fn_x4
COPY = mybir.ActivationFunctionType.Copy
MULT = mybir.AluOpType.mult
ADD = mybir.AluOpType.add
MAX = mybir.AluOpType.max

P = 128
SLOTS = 128
TILES = J // SLOTS
SMALL = -0.3
GAIN = 1.0 - SMALL
THREE = (2,)

LOW_CUTS = (0, 512, 1024)
HIGH_CUTS = (0, 384, 768, 1024)


def tile_moe_expert_heads_twice_pl_kernel(tc, xt, wa_words, wa_scales, wb_words, wb_scales, offs, offs2, out_0, out_1, out_2):
    nc = tc.nc
    with ExitStack() as ctx:
        sb = ctx.enter_context(tc.tile_pool(name="sb", bufs=1))
        ps = ctx.enter_context(tc.psum_pool(name="ps", bufs=1))

        lists = [sb.tile([P, J // 16], U16, name="list%d" % e) for e in range(2)]
        cuts = (LOW_CUTS, HIGH_CUTS)
        raw = [[sb.tile([P, 2, cuts[h][i + 1] - cuts[h][i]], F32, name="raw%d%d" % (h, i)) for i in range(len(cuts[h]) - 1)] for h in range(2)]
        pairs = [sb.tile([P, T], U32, name="pairs%d" % h) for h in range(2)]
        wa = sb.tile([P, 2 * N], U8, name="wa", align_bytes=64)
        wb = sb.tile([P, 4 * N], U8, name="wb", align_bytes=64)
        wa_plane = sb.tile([P, N], U8, name="wa_plane", align_bytes=64)
        wb_plane = sb.tile([P, N], U8, name="wb_plane", align_bytes=64)
        ident = sb.tile([P, P], F32, name="ident")
        y_plane = sb.tile([P, J], U8, name="y_plane", align_bytes=64)

        x_rows = xt.rearrange("(p t) c -> p t c", t=4)

        def load_x(h, i):
            nc.sync.dma_start(out=raw[h][i][:], in_=x_rows[:, 2 * h : 2 * h + 2, cuts[h][i] : cuts[h][i + 1]])

        def load_scales(queue, plane, scales, q):
            queue.dma_start(out=plane[32 * q : 32 * q + 4, :].bitcast(I32), in_=scales[0, 4 * q : 4 * q + 4, :].bitcast(I32))

        nc.gpsimd.memset(wb_plane[:].bitcast(I32), 0)
        nc.gpsimd.memset(wa_plane[:].bitcast(I32), 0)
        nc.sync.dma_start(lists[0][:], offs)
        load_x(0, 0)
        nc.sync.dma_start(lists[1][:], offs2)
        for q in range(4):
            load_scales(nc.sync, wb_plane, wb_scales, q)
        load_x(0, 1)
        for i in range(len(HIGH_CUTS) - 1):
            load_x(1, i)
        nc.sync.dma_start(out=wb[:].bitcast(I32), in_=wb_words[0].rearrange("p n t -> p (n t)").bitcast(I32))
        nc.sync.dma_start(out=wa[:].bitcast(I32), in_=wa_words[0].bitcast(I32))
        for q in range(4):
            load_scales(nc.sync, wa_plane, wa_scales, q)
        make_identity(nc, ident[:])

        def pair_up(engine, h, i, lo, hi):
            dst = pairs[h][:].bitcast(BF16).rearrange("p (c e) -> p c e", e=2)[:, lo:hi, :]
            src = raw[h][i][:, :, lo - cuts[h][i] : hi - cuts[h][i]].rearrange("p e c -> p c e")
            if engine == "vector":
                nc.vector.tensor_copy(out=dst, in_=src)
            else:
                nc.scalar.activation(out=dst, in_=src, func=COPY)

        pair_up("vector", 0, 0, 0, 512)
        pair_up("scalar", 0, 1, 512, 672)
        pair_up("vector", 0, 1, 672, 1024)
        for i in range(len(HIGH_CUTS) - 1):
            pair_up("scalar", 1, i, HIGH_CUTS[i], HIGH_CUTS[i + 1])

        W = 2 * SLOTS
        picked = [sb.tile([P, 4 * W], U32, name="picked%d" % g, align_bytes=64) for g in range(2)]
        quads = {0: picked[1][:, 2 * W :]}

        def gather(h, c, count=1):
            for e in range(2):
                lo = h * 2 * W + e * W + c % 2 * SLOTS
                nc.vector.tensor_copy(out=picked[c // 2][:, lo : lo + count * SLOTS],
                                      in_=pairs[h][:].indirect(lists[e][:, c * 8 : (c + count) * 8]))

        gather(0, 0, 2)
        gather(0, 2, 2)

        x_words = [sb.tile([P, W], U32, name="x_words%d" % c, tag="words%d" % c, align_bytes=64) for c in range(TILES)]
        x_plane = [sb.tile([P, W], U8, name="x_plane%d" % c, align_bytes=64) for c in range(TILES)]
        y_rows = out_0.rearrange("(p t) j -> p t j", t=4)
        p_banks, q_banks, q_small, y_banks = {}, {}, {}, {}
        y_quads = [sb.tile([P, W, 4], BF16, name="y_quads%d" % g, align_bytes=64) for g in range(2)]
        ys = [sb.tile([P, 4, SLOTS], F32, name="y%d" % c) for c in range(TILES)]

        def weave(c, engine, tag=None, es=slice(0, 2)):
            if tag is not None:
                quads[c] = sb.tile([P, 2 * W], U32, name="quads%d" % c, tag=tag, align_bytes=64)[:]
            src = picked[c // 2][:].rearrange("p (h e j) -> p e j h", h=2, e=2)[:, es, c % 2 * SLOTS : (c % 2 + 1) * SLOTS, :]
            dst = quads[c].rearrange("p (e j h) -> p e j h", h=2, e=2)[:, es]
            if engine == "vector":
                nc.vector.tensor_copy(out=dst.bitcast(I32), in_=src.bitcast(I32))
            else:
                nc.scalar.copy(out=dst, in_=src)

        def quantise_x(c):
            nc.vector.quantize_mx(out=x_words[c][:].bitcast(FP8X4), scales=x_plane[c][:], in_=quads[c].bitcast(BF16))

        def multiply(c):
            p_banks[c] = ps.tile([P, N], F32, name="p_bank", tag="p%d" % c)
            q_banks[c] = ps.tile([P, N], F32, name="q_bank", tag="q%d" % c)
            nc.tensor.matmul_mx(out=q_banks[c][:], lhsT=x_words[c][:, SLOTS:].bitcast(FP8X4), lhsT_scale=x_plane[c][:, SLOTS:],
                                rhs=wb[:].bitcast(FP8X4), rhs_scale=wb_plane[:], start=True, stop=True)
            nc.tensor.matmul_mx(out=p_banks[c][:], lhsT=x_words[c][:, :SLOTS].bitcast(FP8X4), lhsT_scale=x_plane[c][:, :SLOTS],
                                rhs=wa[:].bitcast(FP4X4), rhs_scale=wa_plane[:], start=True, stop=True)

        def dealt(bank):
            return bank[:].rearrange("j (m t) -> j t m", t=4)

        def scale_q(c):
            q_small[c] = sb.tile([P, 4, P], F32, name="q_small%d" % c)
            nc.scalar.activation(out=q_small[c][:], in_=dealt(q_banks[c]), func=COPY, scale=SMALL / GAIN if c in THREE else SMALL)

        def turn(c, ts, term, first, last):
            count = ts.stop - ts.start
            for t in range(count):
                nc.tensor.matmul(out=y_banks[c, ts.start][:, t, :], lhsT=term[:, t, :], rhs=ident[:], is_transpose=True,
                                 start=(first and t == 0), stop=(last and t == count - 1))

        def lesser(c, ts, tag):
            count = ts.stop - ts.start
            term = sb.tile([P, count, P], F32, name="lesser%d%d" % (c, ts.start))
            nc.vector.scalar_tensor_tensor(out=term[:], in0=dealt(p_banks[c])[:, ts, :], scalar=SMALL, in1=q_small[c][:, ts, :], op0=MULT, op1=MAX)
            y_banks[c, ts.start] = ps.tile([P, count, SLOTS], F32, name="y_bank", tag=tag)
            turn(c, ts, term, True, False)

        def scale_p(c, tag):
            term = sb.tile([P, 4, P], F32, name="p_small%d" % c)
            nc.scalar.activation(out=term[:], in_=dealt(p_banks[c]), func=COPY, scale=SMALL / GAIN)
            y_banks[c, 0] = ps.tile([P, 4, SLOTS], F32, name="y_bank", tag=tag)
            turn(c, whole, q_small[c], True, False)
            turn(c, whole, term, False, False)

        def greater(c, ts):
            count = ts.stop - ts.start
            term = sb.tile([P, count, P], F32, name="greater", tag="greater%d%d" % (c, ts.start), align_bytes=64)
            nc.vector.scalar_tensor_tensor(out=term[:], in0=q_small[c][:, ts, :], scalar=GAIN / SMALL if c in THREE else 1.0 / SMALL, in1=dealt(p_banks[c])[:, ts, :], op0=MULT, op1=MAX)
            turn(c, ts, term, False, True)

        def copy_y(c, ts):
            if c in THREE:
                nc.scalar.activation(out=ys[c][:, ts, :], in_=y_banks[c, ts.start][:], func=COPY, scale=GAIN)
            else:
                nc.scalar.copy(out=ys[c][:, ts, :], in_=y_banks[c, ts.start][:])
            nc.sync.dma_start(out=y_rows[:, ts, c * SLOTS : (c + 1) * SLOTS], in_=ys[c][:, ts, :])

        def round_y(c, engine):
            src = ys[c][:].rearrange("p t (b i) -> p b t i", i=4)
            dst = y_quads[c // 2][:, c % 2 * SLOTS : (c % 2 + 1) * SLOTS, :].rearrange("p (b i) t -> p b t i", i=4)
            if engine == "vector":
                nc.vector.tensor_copy(out=dst, in_=src)
            elif engine == "gpsimd":
                nc.gpsimd.tensor_scalar(out=dst, in0=src, scalar1=1.0, scalar2=0.0, op0=MULT, op1=ADD)
            else:
                nc.scalar.copy(out=dst, in_=src)

        def round_half(c, ts, src):
            dst = y_quads[c // 2][:, c % 2 * SLOTS : (c % 2 + 1) * SLOTS, ts]
            nc.vector.tensor_copy(out=dst, in_=src.rearrange("p t j -> p j t"))

        def quantise_y(g):
            cols = slice(g * W, (g + 1) * W)
            nc.vector.quantize_mx(out=y_words[:, cols].bitcast(FP8X4), scales=y_plane[:, cols],
                                  in_=y_quads[g][:].rearrange("p j t -> p (j t)"))
            nc.sync.dma_start(out=out_1[0].rearrange("p j t -> p (j t)").bitcast(I32)[:, cols], in_=y_words[:, cols].bitcast(I32))

        whole, low, high = slice(0, 4), slice(0, 2), slice(2, 4)

        gather(1, 0)
        weave(0, "scalar", es=slice(0, 1))
        weave(0, "scalar", es=slice(1, 2))
        gather(1, 1)
        weave(1, "scalar", "quads1")
        quantise_x(0)
        multiply(0)
        gather(1, 2)
        weave(2, "scalar", "quads2")
        quantise_x(1)
        multiply(1)
        scale_q(0)
        gather(1, 3)
        weave(3, "scalar", "quads3")
        quantise_x(2)
        multiply(2)
        scale_q(1)
        lesser(0, whole, "q0")
        quantise_x(3)
        multiply(3)
        greater(0, whole)
        scale_q(2)
        scale_p(2, "q2")
        lesser(1, whole, "q1")
        greater(1, whole)
        copy_y(0, whole)
        round_y(0, "gpsimd")
        scale_q(3)
        greater(2, whole)
        copy_y(1, whole)
        round_y(1, "gpsimd")
        lesser(3, low, "q3")
        greater(3, low)
        lesser(3, high, "p0")
        greater(3, high)
        y_words = sb.tile([P, J], U32, name="y_words", tag="greater32", align_bytes=64)
        copy_y(2, whole)
        round_y(2, "scalar")
        round_half(3, low, y_banks[3, 0][:])
        round_half(3, high, y_banks[3, 2][:])
        copy_y(3, low)
        copy_y(3, high)
        quantise_y(0)
        quantise_y(1)
        for q in range(4):
            queue = nc.sync if q % 2 == 0 else nc.scalar
            queue.dma_start(out=out_2[0, 4 * q : 4 * q + 4, :].bitcast(I32), in_=y_plane[32 * q : 32 * q + 4, :].bitcast(I32))
